import numpy as np
import ml_dtypes


def mxq(x, axis, fmt="e4m3"):
    dtype, down = {"e4m3": (ml_dtypes.float8_e4m3fn, 7), "e5m2": (ml_dtypes.float8_e5m2, 14)}[fmt]
    v = np.moveaxis(np.asarray(x, np.float32).astype(ml_dtypes.bfloat16).astype(np.float64), axis, -1)
    blocks = v.reshape(v.shape[:-1] + (-1, 32))
    amax = np.abs(blocks).max(-1, keepdims=True)
    byte = np.maximum(np.where(amax > 0, np.frexp(amax)[1] - 1 + 127, 0) - down, 1)
    scale = np.exp2(byte - 127.0)
    codes = (blocks / scale).astype(np.float32).astype(dtype).astype(np.float64)
    return np.moveaxis((codes * scale).reshape(v.shape), -1, axis)


WIDE = False


def mx_kscale(k):
    if not WIDE:
        return np.ones(k)
    levels = np.array([10, -10, 5, -5, 0])
    if k % 512:
        return np.exp2(np.random.permutation(np.resize(levels, k // 32))).repeat(32)
    a = np.empty((k // 512, 16))
    for p in range(k // 512):
        a[p, :8] = np.random.permutation(np.resize(levels, 8))
        for g in range(8):
            far = levels[np.abs(levels - a[p, g]) >= 10]
            a[p, g + 8] = far[np.random.randint(len(far))]
    return np.exp2(a.ravel()).repeat(32)


def f64(x):
    return np.asarray(x).astype(np.float64)


def striped(idx):
    return np.tile(np.asarray(idx).reshape(-1, 16).T, (8, 1)).astype(np.uint16)


def unstriped(offs):
    return offs[:16].T.reshape(-1).astype(np.int64)


E2M1 = np.array([0.0, 0.5, 1.0, 1.5, 2.0, 3.0, 4.0, 6.0, -0.0, -0.5, -1.0, -1.5, -2.0, -3.0, -4.0, -6.0])


def pack_weight(w, fmt):
    k, n = w.shape
    w = f64(np.asarray(w, np.float32).astype(ml_dtypes.bfloat16)).reshape(k // 32, 32, n)
    amax = np.abs(w).max(1)
    if fmt == "e4m3":
        byte = np.frexp(amax)[1] - 1 + 127 - 7
    else:
        mant, ex = np.frexp(amax / 6.0)
        byte = np.where(mant > 0.5, ex, ex - 1) + 127
    byte = np.clip(np.where(amax > 0, byte, 1), 1, 254)
    scaled = (w * np.exp2(127.0 - byte)[:, None, :]).reshape(k, n).astype(np.float32)
    by_word = np.ascontiguousarray(scaled.reshape(k // 512, 128, 4, n).transpose(0, 1, 3, 2))
    if fmt == "e4m3":
        words = by_word.astype(ml_dtypes.float8_e4m3fn).view(np.uint8)
    else:
        c = by_word.astype(ml_dtypes.float4_e2m1fn).view(np.uint8) & 0xF
        words = (c[..., 0::2] | (c[..., 1::2] << 4)).reshape(k // 512, 128, 2 * n)
    return np.ascontiguousarray(words), np.ascontiguousarray(byte.astype(np.uint8).reshape(k // 512, 16, n))


def unpack_weight(words, scales, fmt):
    g, _, n = scales.shape
    words = np.ascontiguousarray(words).reshape(g, 128, n, -1)
    if fmt == "e4m3":
        vals = words.view(ml_dtypes.float8_e4m3fn).astype(np.float64)
    else:
        nib = np.empty((g, 128, n, 4), np.uint8)
        nib[..., 0::2] = words & 0xF
        nib[..., 1::2] = words >> 4
        vals = E2M1[nib]
    vals = vals * np.repeat(np.exp2(scales.astype(np.float64) - 127.0), 8, axis=1)[..., None]
    return vals.transpose(0, 1, 3, 2).reshape(g * 512, n)


def sigmoid(v):
    return 1.0 / (1.0 + np.exp(-v))


D, E, T, I, Q = 512, 512, 2048, 512, 128


def setup_inputs():
    n = np.random.standard_normal
    idx = np.random.permutation(T)[:I]
    fd = mx_kscale(D)
    fe = mx_kscale(E)
    keysp = pack_weight(n((D, T)) / fd[:, None], "e2m1")
    valsp = pack_weight(n((E, T)) / fe[:, None], "e2m1")
    return {
        "query": (n((D, Q)) * 0.8 / np.sqrt(D) * fd[:, None]).astype(np.float32),
        "keys_words": keysp[0],
        "keys_scales": keysp[1],
        "th": (np.random.uniform(0.4, 1.0, (Q, 1))).astype(np.float32),
        "gout": (n((E, Q)) * 1 / np.sqrt(E) * fe[:, None]).astype(np.float32),
        "vals_words": valsp[0],
        "vals_scales": valsp[1],
        "dquery": (n((D, Q)) * 1.0 / np.sqrt(D) * fd[:, None]).astype(np.float32),
        "base": (0.5 * n((Q, T))).astype(np.float32),
        "offs": striped(idx),
    }


def reference(query, keys_words, keys_scales, th, gout, vals_words, vals_scales, dquery, base, offs):
    idx = unstriped(offs)
    keysu = unpack_weight(keys_words, keys_scales, "e2m1")
    valsu = unpack_weight(vals_words, vals_scales, "e2m1")
    queryq = mxq(f64(query), 0, "e4m3")
    keysidxg = keysu[:, idx]
    a = queryq.T @ keysidxg
    dqueryq = mxq(f64(dquery), 0, "e4m3")
    ta = dqueryq.T @ keysidxg
    e1s = sigmoid((f64(th) - np.mean(np.square(a), axis=1, keepdims=True)) * 4.0)
    p = np.exp(a - np.max(a, axis=1, keepdims=True))
    z = np.sum(p, axis=1, keepdims=True)
    goutq = mxq(f64(gout), 0, "e4m3")
    valsidxg = valsu[:, idx]
    c0 = goutq.T @ valsidxg
    dz = np.sum(c0 * (1.0 - e1s) * p / np.square(z) * (-1.0), axis=1, keepdims=True)
    dp = c0 * (1.0 - e1s) / z + dz
    de1s = np.sum(c0, axis=1, keepdims=True) / 512.0 - np.sum(c0 * p / z, axis=1, keepdims=True)
    te1s = np.mean(ta * a * 2.0, axis=1, keepdims=True) * (-1.0) * 4.0 * e1s * (1.0 - e1s)
    tp = ta * p
    tz = np.sum(tp, axis=1, keepdims=True)
    tdz = np.sum((te1s * (-1.0) * c0 * p + tp * c0 * (1.0 - e1s) - tz * z * 2.0 * c0 * (1.0 - e1s) * p / np.square(z)) / np.square(z) * (-1.0), axis=1, keepdims=True)
    tdp = (te1s * (-1.0) * c0 - tz * c0 * (1.0 - e1s) / z) / z + tdz
    tde1s = np.sum((tp - tz * p / z) / z * c0, axis=1, keepdims=True) * (-1.0)
    tda = tdp * p + tp * dp + (((tde1s * e1s + te1s * de1s) * (1.0 - e1s) + te1s * (-1.0) * de1s * e1s) * 4.0 * (-1.0) / 512.0 * a + ta * de1s * e1s * (1.0 - e1s) * 4.0 * (-1.0) / 512.0) * 2.0
    gs = tda * 512.0
    gf = np.zeros((Q, T))
    gf[:, idx] = gs
    y = f64(base) + gf
    return y

@@ -1,0 +1,221 @@
+from contextlib import ExitStack
+
+import concourse.mybir as mybir
+
+D, E, T, I, Q = 512, 512, 2048, 512, 128
+FLOPS = 2 * Q * I * (2 * D + E)
+
+F32 = mybir.dt.float32
+BF16 = mybir.dt.bfloat16
+I32 = mybir.dt.int32
+U32 = mybir.dt.uint32
+U16 = mybir.dt.uint16
+U8 = mybir.dt.uint8
+FP8X4 = mybir.dt.float8_e4m3fn_x4
+FP4X4 = mybir.dt.float4_e2m1fn_x4
+ALU = mybir.AluOpType
+ACT = mybir.ActivationFunctionType
+
+P = 128
+PACK = 4
+OUT_EDGES = (0, 256, 768, 1280, 1792, 2048)
+
+
+def tile_attend_hvevenbyspread_s_kernel(
+    tc, query, keys_words, keys_scales, th, gout, vals_words, vals_scales, dquery, base, offs, out
+):
+    nc = tc.nc
+    with ExitStack() as ctx:
+        sb = ctx.enter_context(tc.tile_pool(name="sb", bufs=1))
+        ps = ctx.enter_context(tc.psum_pool(name="ps", bufs=1))
+
+        def column(name, width=1):
+            return sb.tile([P, width], F32, name=name)
+
+        def wide(name, tag=""):
+            return sb.tile([P, I], F32, name=name, tag=tag or name)
+
+        def load_scales(queue, tile, scales):
+            for quad in range(4):
+                queue.dma_start(
+                    out=tile[32 * quad : 32 * quad + 4, :].bitcast(I32),
+                    in_=scales[0, 4 * quad : 4 * quad + 4, :].bitcast(I32),
+                )
+
+        def load_rows(queue, rows, name, tag):
+            raw = sb.tile([P, PACK, Q], F32, name=name, tag=tag)
+            queue.dma_start(out=raw[:], in_=rows.rearrange("(p j) w -> p j w", j=PACK))
+            return raw
+
+        def interleave(raw, name):
+            grouped = sb.tile([P, Q, PACK], BF16, name=name, tag=name, align_bytes=64)
+            nc.scalar.copy(out=grouped[:], in_=raw[:].rearrange("p j w -> p w j"))
+            return grouped
+
+        def quantize(grouped, name):
+            codes = sb.tile([P, Q], U32, name=name + "_codes", align_bytes=64)
+            scales = sb.tile([P, Q], U8, name=name + "_scales", align_bytes=64)
+            nc.vector.quantize_mx(
+                out=codes[:].bitcast(FP8X4), scales=scales[:], in_=grouped[:].rearrange("p w j -> p (w j)")
+            )
+            return codes, scales
+
+        def gather(pool_tile, dtype, name, tag=""):
+            picked = sb.tile([P, I], dtype, name=name, tag=tag or name, align_bytes=64)
+            nc.vector.tensor_copy(picked[:], pool_tile[:].indirect(offsets[:]))
+            return picked
+
+        def product(rows_q, words, scales, name):
+            bank = ps.tile([P, I], F32, name=name)
+            nc.tensor.matmul_mx(
+                out=bank[:],
+                lhsT=rows_q[0][:].bitcast(FP8X4),
+                lhsT_scale=rows_q[1][:],
+                rhs=words[:].bitcast(FP4X4),
+                rhs_scale=scales[:],
+                start=True,
+                stop=True,
+            )
+            return bank
+
+        def fma(dst, x, scale, bias=0.0):
+            nc.scalar.activation(out=dst, in_=x, func=ACT.Identity, scale=scale, bias=bias)
+
+        key_scale_pool = sb.tile([P, T], U8, name="key_scale_pool", tag="key_scale_pool", align_bytes=64)
+        val_scale_pool = sb.tile([P, T], U8, name="val_scale_pool", tag="val_scale_pool")
+        placed = sb.tile([P, T], F32, name="placed")
+        nc.vector.memset(key_scale_pool[:].bitcast(I32), 0)
+        one_a = sb.tile([P, 1], F32, name="one_a", tag="val_word_pool")
+        one_b = sb.tile([P, 1], F32, name="one_b", tag="gout_raw")
+        nc.vector.memset(one_a[:], 1.0)
+        nc.vector.memset(one_b[:], 1.0)
+        inv128 = column("inv128")
+        fma(inv128[:], one_a[:], 1.0 / 128)
+        c256 = column("c256")
+        fma(c256[:], one_b[:], 256.0)
+        nc.vector.memset(placed[:].bitcast(I32), 0)
+        nc.vector.memset(val_scale_pool[:].bitcast(I32), 0)
+
+        offsets = sb.tile([P, I // 16], U16, name="offsets")
+        nc.sync.dma_start(offsets[:], offs)
+        key_word_pool = sb.tile([P, T], U16, name="key_word_pool")
+        nc.sync.dma_start(out=key_word_pool[:].bitcast(I32), in_=keys_words[0].bitcast(I32))
+        query_raw = load_rows(nc.sync, query, "query_raw", "query_raw")
+        dquery_raw = load_rows(nc.sync, dquery, "dquery_raw", "dquery_raw")
+        load_scales(nc.sync, key_scale_pool, keys_scales)
+        val_word_pool = sb.tile([P, T], U16, name="val_word_pool", tag="val_word_pool")
+        nc.sync.dma_start(out=val_word_pool[:].bitcast(I32), in_=vals_words[0].bitcast(I32))
+        gout_raw = load_rows(nc.sync, gout, "gout_raw", "gout_raw")
+        load_scales(nc.sync, val_scale_pool, vals_scales)
+        th_col = column("th_col")
+        nc.gpsimd.dma_start(out=th_col[:], in_=th)
+
+        query_g = interleave(query_raw, "query_g")
+        dquery_g = interleave(dquery_raw, "dquery_g")
+        base_sb = sb.tile([P, T], F32, name="base_sb", tag="dquery_raw")
+        nc.sync.dma_start(out=base_sb[:], in_=base)
+        th2 = column("th2")
+        fma(th2[:], th_col[:], 2.0)
+        key_words = gather(key_word_pool, U16, "key_words")
+        query_q = quantize(query_g, "query_q")
+        key_scales = gather(key_scale_pool, U8, "key_scales")
+        a = product(query_q, key_words, key_scales, "a")
+        dquery_q = quantize(dquery_g, "dquery_q")
+        ta = product(dquery_q, key_words, key_scales, "ta")
+        gout_g = interleave(gout_raw, "gout_g")
+
+        unused_s = wide("unused_s", "gout_raw")
+        sum_a2 = column("sum_a2")
+        nc.scalar.activation(out=unused_s[:], in_=a[:], func=ACT.Square, accum_out=sum_a2[:])
+
+        val_words = gather(val_word_pool, U16, "val_words", "key_scale_pool")
+        neg_a = wide("neg_a", "val_word_pool")
+        neg_max = column("neg_max")
+        nc.vector.tensor_scalar(
+            out=neg_a[:], in0=a[:], scalar1=-1.0, scalar2=None, op0=ALU.mult, op1=ALU.min, accum_out=neg_max[:]
+        )
+        gout_q = quantize(gout_g, "gout_q")
+        val_scales = gather(val_scale_pool, U8, "val_scales", "gout_g")
+        c0 = product(gout_q, val_words, val_scales, "c0")
+
+        p = wide("p")
+        z = column("z")
+        nc.scalar.activation(out=p[:], in_=neg_a[:], func=ACT.Exp, scale=-1.0, bias=neg_max[:], accum_out=z[:])
+        scratch = sb.tile([P, I + 8], F32, name="scratch", tag="val_scale_pool")
+        unused_v, rnt = scratch[:, 0:I], scratch[:, I : I + 3]
+        r, neg_r, tanh = rnt[:, 0:1], rnt[:, 1:2], rnt[:, 2:3]
+        nc.scalar.activation(out=tanh, in_=sum_a2[:], func=ACT.Tanh, scale=-2.0 / I, bias=th2[:])
+        s64 = column("s64")
+        fma(s64[:], tanh, 1.0 / 128, inv128[:])
+        u512 = column("u512")
+        fma(u512[:], tanh, -256.0, c256[:])
+
+        nc.vector.reciprocal(out=r, in_=z[:])
+        neg_ta_a = column("neg_ta_a")
+        nc.vector.scalar_tensor_tensor(
+            out=unused_v, in0=ta[:], scalar=1.0, in1=neg_a[:], op0=ALU.mult, op1=ALU.mult, accum_out=neg_ta_a[:]
+        )
+        t = column("t")
+        nc.vector.scalar_tensor_tensor(
+            out=unused_v, in0=ta[:], scalar=r, in1=p[:], op0=ALU.mult, op1=ALU.mult, accum_out=t[:]
+        )
+        fma(neg_r, r, -1.0)
+        kcols = column("kcols", 4)
+        fma(kcols[:, 3:4], z[:], 64.0)
+        fma(kcols[:, 0:3], rnt, u512[:])
+        k3, neg_k3 = kcols[:, 0:1], kcols[:, 1:2]
+        by_s = column("by_s", 3)
+        fma(by_s[:], kcols[:, 1:4], s64[:])
+        fma(by_s[:, 0:2], by_s[:, 0:2], neg_ta_a[:])
+
+        c_part = column("c_part")
+        nc.scalar.activation(out=unused_s[:], in_=c0[:], func=ACT.Copy, scale=1.0 / (64 * I), accum_out=c_part[:])
+
+        sx_beta = column("sx_beta", 2)
+        fma(sx_beta[:, 1:2], t[:], neg_k3, by_s[:, 0:1])
+        x = wide("x")
+        nc.scalar.activation(
+            out=x[:], in_=ta[:], func=ACT.Identity, scale=k3, bias=sx_beta[:, 1:2], accum_out=sx_beta[:, 0:1]
+        )
+
+        m = column("m")
+        nc.vector.scalar_tensor_tensor(
+            out=unused_v, in0=c0[:], scalar=r, in1=p[:], op0=ALU.mult, op1=ALU.mult, accum_out=m[:]
+        )
+        q = wide("q")
+        nc.vector.scalar_tensor_tensor(out=q[:], in0=c0[:], scalar=m[:], in1=p[:], op0=ALU.subtract, op1=ALU.mult)
+
+        de64 = column("de64")
+        fma(de64[:], m[:], -1.0 / 64, c_part[:])
+        c1_nk = column("c1_nk", 2)
+        fma(c1_nk[:], by_s[:, 1:3], de64[:])
+        c1, neg_kappa = c1_nk[:, 0:1], c1_nk[:, 1:2]
+        h = wide("h")
+        sum_h = column("sum_h")
+        nc.vector.scalar_tensor_tensor(
+            out=h[:], in0=q[:], scalar=neg_kappa, in1=x[:], op0=ALU.subtract, op1=ALU.mult, accum_out=sum_h[:]
+        )
+        by_kappa = column("by_kappa", 2)
+        fma(by_kappa[:], sx_beta[:], neg_kappa)
+        k0 = column("k0")
+        fma(k0[:], by_kappa[:, 0:1], s64[:], c1)
+
+        gamma = column("gamma")
+        nc.vector.tensor_scalar(
+            out=gamma[:], in0=sum_h[:], scalar1=by_kappa[:, 0:1], scalar2=neg_r, op0=ALU.add, op1=ALU.mult
+        )
+        k5 = column("k5")
+        fma(k5[:], sum_h[:], s64[:], k0[:])
+        v_a = wide("v_a")
+        fma(v_a[:], a[:], k5[:], by_kappa[:, 1:2])
+        v_p = wide("v_p")
+        nc.vector.scalar_tensor_tensor(out=v_p[:], in0=p[:], scalar=gamma[:], in1=h[:], op0=ALU.mult, op1=ALU.add)
+
+        nc.vector.tensor_tensor(placed[:].indirect(offsets[:]), v_p[:], v_a[:], ALU.add)
+
+        for n in range(len(OUT_EDGES) - 1):
+            cols = slice(OUT_EDGES[n], OUT_EDGES[n + 1])
+            total = sb.tile([P, cols.stop - cols.start], F32, name=f"total{n}")
+            nc.vector.tensor_tensor(total[:], placed[:, cols], base_sb[:, cols], ALU.add)
+            queue = nc.sync if n % 2 == 0 else nc.scalar
+            queue.dma_start(out=out[:, cols], in_=total[:])

@@ -90,9 +90,11 @@ def tile_attend_hvevenbyspread_s_kernel(
         nc.vector.memset(one_a[:], 1.0)
         nc.vector.memset(one_b[:], 1.0)
         inv128 = column("inv128")
-        fma(inv128[:], one_a[:], 1.0 / 128)
+        nc.vector.tensor_scalar_mul(inv128[:], one_a[:], 1.0 / 128)
         c256 = column("c256")
         fma(c256[:], one_b[:], 256.0)
+        by_r_in = column("by_r_in", 4)
+        nc.vector.memset(by_r_in[:, 2:3], -1.0)
         nc.vector.memset(placed[:].bitcast(I32), 0)
         nc.vector.memset(val_scale_pool[:].bitcast(I32), 0)
 
@@ -102,7 +104,7 @@ def tile_attend_hvevenbyspread_s_kernel(
         nc.sync.dma_start(out=key_word_pool[:].bitcast(I32), in_=keys_words[0].bitcast(I32))
         query_raw = load_rows(nc.sync, query, "query_raw", "query_raw")
         dquery_raw = load_rows(nc.sync, dquery, "dquery_raw", "dquery_raw")
-        load_scales(nc.sync, key_scale_pool, keys_scales)
+        load_scales(nc.scalar, key_scale_pool, keys_scales)
         val_word_pool = sb.tile([P, T], U16, name="val_word_pool", tag="val_word_pool")
         nc.sync.dma_start(out=val_word_pool[:].bitcast(I32), in_=vals_words[0].bitcast(I32))
         gout_raw = load_rows(nc.sync, gout, "gout_raw", "gout_raw")
@@ -129,67 +131,77 @@ def tile_attend_hvevenbyspread_s_kernel(
         nc.scalar.activation(out=unused_s[:], in_=a[:], func=ACT.Square, accum_out=sum_a2[:])
 
         val_words = gather(val_word_pool, U16, "val_words", "key_scale_pool")
+        gout_q = quantize(gout_g, "gout_q")
         neg_a = wide("neg_a", "val_word_pool")
         neg_max = column("neg_max")
         nc.vector.tensor_scalar(
             out=neg_a[:], in0=a[:], scalar1=-1.0, scalar2=None, op0=ALU.mult, op1=ALU.min, accum_out=neg_max[:]
         )
-        gout_q = quantize(gout_g, "gout_q")
         val_scales = gather(val_scale_pool, U8, "val_scales", "gout_g")
         c0 = product(gout_q, val_words, val_scales, "c0")
 
         p = wide("p")
         z = column("z")
         nc.scalar.activation(out=p[:], in_=neg_a[:], func=ACT.Exp, scale=-1.0, bias=neg_max[:], accum_out=z[:])
-        scratch = sb.tile([P, I + 8], F32, name="scratch", tag="val_scale_pool")
-        unused_v, rnt = scratch[:, 0:I], scratch[:, I : I + 3]
-        r, neg_r, tanh = rnt[:, 0:1], rnt[:, 1:2], rnt[:, 2:3]
-        nc.scalar.activation(out=tanh, in_=sum_a2[:], func=ACT.Tanh, scale=-2.0 / I, bias=th2[:])
-        s64 = column("s64")
-        fma(s64[:], tanh, 1.0 / 128, inv128[:])
-        u512 = column("u512")
-        fma(u512[:], tanh, -256.0, c256[:])
 
+        tanh = column("tanh")
+        nc.scalar.activation(out=tanh[:], in_=sum_a2[:], func=ACT.Tanh, scale=-2.0 / I, bias=th2[:])
+        s64 = column("s64")
+        fma(s64[:], tanh[:], 1.0 / 128, inv128[:])
+        fma(by_r_in[:, 0:1], tanh[:], -256.0, c256[:])
+        fma(by_r_in[:, 1:2], by_r_in[:, 0:1], -1.0)
+        fma(by_r_in[:, 3:4], by_r_in[:, 1:2], s64[:])
+        neg_tanh64 = column("neg_tanh64")
+        fma(neg_tanh64[:], tanh[:], -1.0 / 64)
+        by_r = column("by_r", 5)
+        fma(by_r[:, 4:5], by_r_in[:, 3:4], neg_tanh64[:])
+        coef = column("coef", 3)
+        fma(coef[:, 2:3], s64[:], z[:])
+
+        scratch = sb.tile([P, I + 8], F32, name="scratch", tag="val_scale_pool")
+        r = scratch[:, I : I + 1]
         nc.vector.reciprocal(out=r, in_=z[:])
         neg_ta_a = column("neg_ta_a")
         nc.vector.scalar_tensor_tensor(
-            out=unused_v, in0=ta[:], scalar=1.0, in1=neg_a[:], op0=ALU.mult, op1=ALU.mult, accum_out=neg_ta_a[:]
+            out=scratch[:, 0:I], in0=ta[:], scalar=1.0, in1=neg_a[:], op0=ALU.mult, op1=ALU.mult, accum_out=neg_ta_a[:]
         )
         t = column("t")
+        unused_t = wide("unused_t")
         nc.vector.scalar_tensor_tensor(
-            out=unused_v, in0=ta[:], scalar=r, in1=p[:], op0=ALU.mult, op1=ALU.mult, accum_out=t[:]
+            out=unused_t[:], in0=ta[:], scalar=r, in1=p[:], op0=ALU.mult, op1=ALU.mult, accum_out=t[:]
         )
-        fma(neg_r, r, -1.0)
-        kcols = column("kcols", 4)
-        fma(kcols[:, 3:4], z[:], 64.0)
-        fma(kcols[:, 0:3], rnt, u512[:])
-        k3, neg_k3 = kcols[:, 0:1], kcols[:, 1:2]
-        by_s = column("by_s", 3)
-        fma(by_s[:], kcols[:, 1:4], s64[:])
-        fma(by_s[:, 0:2], by_s[:, 0:2], neg_ta_a[:])
+        fma(by_r[:, 0:4], by_r_in[:], r)
+        k3, neg_k3, neg_r = by_r[:, 0:1], by_r[:, 1:2], by_r[:, 2:3]
+        fma(coef[:, 0:2], by_r[:, 3:5], neg_ta_a[:])
 
-        c_part = column("c_part")
-        nc.scalar.activation(out=unused_s[:], in_=c0[:], func=ACT.Copy, scale=1.0 / (64 * I), accum_out=c_part[:])
+        c_mean = column("c_mean")
+        unused_c = wide("unused_c")
+        nc.scalar.activation(out=unused_c[:], in_=c0[:], func=ACT.Copy, scale=1.0 / I, accum_out=c_mean[:])
 
         sx_beta = column("sx_beta", 2)
-        fma(sx_beta[:, 1:2], t[:], neg_k3, by_s[:, 0:1])
+        fma(sx_beta[:, 1:2], t[:], neg_k3, coef[:, 0:1])
         x = wide("x")
         nc.scalar.activation(
             out=x[:], in_=ta[:], func=ACT.Identity, scale=k3, bias=sx_beta[:, 1:2], accum_out=sx_beta[:, 0:1]
         )
 
         m = column("m")
+        unused_m = wide("unused_m")
         nc.vector.scalar_tensor_tensor(
-            out=unused_v, in0=c0[:], scalar=r, in1=p[:], op0=ALU.mult, op1=ALU.mult, accum_out=m[:]
+            out=unused_m[:], in0=c0[:], scalar=r, in1=p[:], op0=ALU.mult, op1=ALU.mult, accum_out=m[:]
         )
+        c1_nk = column("c1_nk", 2)
+        nc.vector.scalar_tensor_tensor(
+            out=c1_nk[:],
+            in0=c_mean[:].to_broadcast([P, 2]),
+            scalar=m[:],
+            in1=coef[:, 1:3],
+            op0=ALU.subtract,
+            op1=ALU.mult,
+        )
+        c1, neg_kappa = c1_nk[:, 0:1], c1_nk[:, 1:2]
         q = wide("q")
         nc.vector.scalar_tensor_tensor(out=q[:], in0=c0[:], scalar=m[:], in1=p[:], op0=ALU.subtract, op1=ALU.mult)
-
-        de64 = column("de64")
-        fma(de64[:], m[:], -1.0 / 64, c_part[:])
-        c1_nk = column("c1_nk", 2)
-        fma(c1_nk[:], by_s[:, 1:3], de64[:])
-        c1, neg_kappa = c1_nk[:, 0:1], c1_nk[:, 1:2]
         h = wide("h")
         sum_h = column("sum_h")
         nc.vector.scalar_tensor_tensor(

@@ -82,21 +82,16 @@ def tile_attend_hvevenbyspread_s_kernel(
             nc.scalar.activation(out=dst, in_=x, func=ACT.Identity, scale=scale, bias=bias)
 
         key_scale_pool = sb.tile([P, T], U8, name="key_scale_pool", tag="key_scale_pool", align_bytes=64)
-        val_scale_pool = sb.tile([P, T], U8, name="val_scale_pool", tag="val_scale_pool")
-        placed = sb.tile([P, T], F32, name="placed")
         nc.vector.memset(key_scale_pool[:].bitcast(I32), 0)
         one_a = sb.tile([P, 1], F32, name="one_a", tag="val_word_pool")
         one_b = sb.tile([P, 1], F32, name="one_b", tag="gout_raw")
         nc.vector.memset(one_a[:], 1.0)
         nc.vector.memset(one_b[:], 1.0)
+        factor = sb.tile([P, 1], F32, name="factor", tag="val_scale_pool")
+        nc.vector.memset(factor[:], 256.0)
         inv128 = column("inv128")
         nc.vector.tensor_scalar_mul(inv128[:], one_a[:], 1.0 / 128)
-        c256 = column("c256")
-        fma(c256[:], one_b[:], 256.0)
         by_r_in = column("by_r_in", 4)
-        nc.vector.memset(by_r_in[:, 2:3], -1.0)
-        nc.vector.memset(placed[:].bitcast(I32), 0)
-        nc.vector.memset(val_scale_pool[:].bitcast(I32), 0)
 
         offsets = sb.tile([P, I // 16], U16, name="offsets")
         nc.sync.dma_start(offsets[:], offs)
@@ -105,6 +100,11 @@ def tile_attend_hvevenbyspread_s_kernel(
         query_raw = load_rows(nc.sync, query, "query_raw", "query_raw")
         dquery_raw = load_rows(nc.sync, dquery, "dquery_raw", "dquery_raw")
         load_scales(nc.scalar, key_scale_pool, keys_scales)
+        c256 = column("c256")
+        nc.scalar.copy(out=c256[:], in_=factor[:])
+        fma(by_r_in[:, 2:3], one_b[:], -1.0)
+        val_scale_pool = sb.tile([P, T], U8, name="val_scale_pool", tag="val_scale_pool")
+        nc.vector.memset(val_scale_pool[:].bitcast(I32), 0)
         val_word_pool = sb.tile([P, T], U16, name="val_word_pool", tag="val_word_pool")
         nc.sync.dma_start(out=val_word_pool[:].bitcast(I32), in_=vals_words[0].bitcast(I32))
         gout_raw = load_rows(nc.sync, gout, "gout_raw", "gout_raw")
@@ -139,6 +139,9 @@ def tile_attend_hvevenbyspread_s_kernel(
         )
         val_scales = gather(val_scale_pool, U8, "val_scales", "gout_g")
         c0 = product(gout_q, val_words, val_scales, "c0")
+
+        placed = sb.tile([P, T], F32, name="placed", tag="gout_g", align_bytes=64)
+        nc.gpsimd.memset(placed[:], 0.0)
 
         p = wide("p")
         z = column("z")

from contextlib import ExitStack

import concourse.mybir as mybir

D, E, T, I, Q = 512, 512, 2048, 512, 128
FLOPS = 2 * Q * I * (2 * D + E)

F32 = mybir.dt.float32
BF16 = mybir.dt.bfloat16
I32 = mybir.dt.int32
U32 = mybir.dt.uint32
U16 = mybir.dt.uint16
U8 = mybir.dt.uint8
FP8X4 = mybir.dt.float8_e4m3fn_x4
FP4X4 = mybir.dt.float4_e2m1fn_x4
ALU = mybir.AluOpType
ACT = mybir.ActivationFunctionType

P = 128
PACK = 4
OUT_EDGES = (0, 256, 768, 1280, 1792, 2048)


def tile_attend_hvevenbyspread_s_kernel(
    tc, query, keys_words, keys_scales, th, gout, vals_words, vals_scales, dquery, base, offs, out
):
    nc = tc.nc
    with ExitStack() as ctx:
        sb = ctx.enter_context(tc.tile_pool(name="sb", bufs=1))
        ps = ctx.enter_context(tc.psum_pool(name="ps", bufs=1))

        def column(name, width=1):
            return sb.tile([P, width], F32, name=name)

        def wide(name, tag=""):
            return sb.tile([P, I], F32, name=name, tag=tag or name)

        def load_scales(queue, tile, scales):
            for quad in range(4):
                queue.dma_start(
                    out=tile[32 * quad : 32 * quad + 4, :].bitcast(I32),
                    in_=scales[0, 4 * quad : 4 * quad + 4, :].bitcast(I32),
                )

        def load_rows(queue, rows, name, tag):
            raw = sb.tile([P, PACK, Q], F32, name=name, tag=tag)
            queue.dma_start(out=raw[:], in_=rows.rearrange("(p j) w -> p j w", j=PACK))
            return raw

        def interleave(raw, name):
            grouped = sb.tile([P, Q, PACK], BF16, name=name, tag=name, align_bytes=64)
            nc.scalar.copy(out=grouped[:], in_=raw[:].rearrange("p j w -> p w j"))
            return grouped

        def quantize(grouped, name):
            codes = sb.tile([P, Q], U32, name=name + "_codes", align_bytes=64)
            scales = sb.tile([P, Q], U8, name=name + "_scales", align_bytes=64)
            nc.vector.quantize_mx(
                out=codes[:].bitcast(FP8X4), scales=scales[:], in_=grouped[:].rearrange("p w j -> p (w j)")
            )
            return codes, scales

        def gather(pool_tile, dtype, name, tag=""):
            picked = sb.tile([P, I], dtype, name=name, tag=tag or name, align_bytes=64)
            nc.vector.tensor_copy(picked[:], pool_tile[:].indirect(offsets[:]))
            return picked

        def product(rows_q, words, scales, name):
            bank = ps.tile([P, I], F32, name=name)
            nc.tensor.matmul_mx(
                out=bank[:],
                lhsT=rows_q[0][:].bitcast(FP8X4),
                lhsT_scale=rows_q[1][:],
                rhs=words[:].bitcast(FP4X4),
                rhs_scale=scales[:],
                start=True,
                stop=True,
            )
            return bank

        def fma(dst, x, scale, bias=0.0):
            nc.scalar.activation(out=dst, in_=x, func=ACT.Identity, scale=scale, bias=bias)

        key_scale_pool = sb.tile([P, T], U8, name="key_scale_pool", tag="key_scale_pool", align_bytes=64)
        nc.vector.memset(key_scale_pool[:].bitcast(I32), 0)
        one_a = sb.tile([P, 1], F32, name="one_a", tag="val_word_pool")
        one_b = sb.tile([P, 1], F32, name="one_b", tag="gout_raw")
        nc.vector.memset(one_a[:], 1.0)
        nc.vector.memset(one_b[:], 1.0)
        factor = sb.tile([P, 1], F32, name="factor", tag="val_scale_pool")
        nc.vector.memset(factor[:], 256.0)
        inv128 = column("inv128")
        nc.vector.tensor_scalar_mul(inv128[:], one_a[:], 1.0 / 128)
        by_r_in = column("by_r_in", 4)

        offsets = sb.tile([P, I // 16], U16, name="offsets")
        nc.sync.dma_start(offsets[:], offs)
        key_word_pool = sb.tile([P, T], U16, name="key_word_pool")
        nc.sync.dma_start(out=key_word_pool[:].bitcast(I32), in_=keys_words[0].bitcast(I32))
        query_raw = load_rows(nc.sync, query, "query_raw", "query_raw")
        dquery_raw = load_rows(nc.sync, dquery, "dquery_raw", "dquery_raw")
        load_scales(nc.scalar, key_scale_pool, keys_scales)
        c256 = column("c256")
        nc.scalar.copy(out=c256[:], in_=factor[:])
        fma(by_r_in[:, 2:3], one_b[:], -1.0)
        val_scale_pool = sb.tile([P, T], U8, name="val_scale_pool", tag="val_scale_pool")
        nc.vector.memset(val_scale_pool[:].bitcast(I32), 0)
        val_word_pool = sb.tile([P, T], U16, name="val_word_pool", tag="val_word_pool")
        nc.sync.dma_start(out=val_word_pool[:].bitcast(I32), in_=vals_words[0].bitcast(I32))
        gout_raw = load_rows(nc.sync, gout, "gout_raw", "gout_raw")
        load_scales(nc.sync, val_scale_pool, vals_scales)
        th_col = column("th_col")
        nc.gpsimd.dma_start(out=th_col[:], in_=th)

        query_g = interleave(query_raw, "query_g")
        dquery_g = interleave(dquery_raw, "dquery_g")
        base_sb = sb.tile([P, T], F32, name="base_sb", tag="dquery_raw")
        nc.sync.dma_start(out=base_sb[:], in_=base)
        th2 = column("th2")
        fma(th2[:], th_col[:], 2.0)
        key_words = gather(key_word_pool, U16, "key_words")
        query_q = quantize(query_g, "query_q")
        key_scales = gather(key_scale_pool, U8, "key_scales")
        a = product(query_q, key_words, key_scales, "a")
        dquery_q = quantize(dquery_g, "dquery_q")
        ta = product(dquery_q, key_words, key_scales, "ta")
        gout_g = interleave(gout_raw, "gout_g")

        unused_s = wide("unused_s", "gout_raw")
        sum_a2 = column("sum_a2")
        nc.scalar.activation(out=unused_s[:], in_=a[:], func=ACT.Square, accum_out=sum_a2[:])

        val_words = gather(val_word_pool, U16, "val_words", "key_scale_pool")
        gout_q = quantize(gout_g, "gout_q")
        neg_a = wide("neg_a", "val_word_pool")
        neg_max = column("neg_max")
        nc.vector.tensor_scalar(
            out=neg_a[:], in0=a[:], scalar1=-1.0, scalar2=None, op0=ALU.mult, op1=ALU.min, accum_out=neg_max[:]
        )
        val_scales = gather(val_scale_pool, U8, "val_scales", "gout_g")
        c0 = product(gout_q, val_words, val_scales, "c0")

        placed = sb.tile([P, T], F32, name="placed", tag="gout_g", align_bytes=64)
        nc.gpsimd.memset(placed[:], 0.0)

        p = wide("p")
        z = column("z")
        nc.scalar.activation(out=p[:], in_=neg_a[:], func=ACT.Exp, scale=-1.0, bias=neg_max[:], accum_out=z[:])

        tanh = column("tanh")
        nc.scalar.activation(out=tanh[:], in_=sum_a2[:], func=ACT.Tanh, scale=-2.0 / I, bias=th2[:])
        s64 = column("s64")
        fma(s64[:], tanh[:], 1.0 / 128, inv128[:])
        fma(by_r_in[:, 0:1], tanh[:], -256.0, c256[:])
        fma(by_r_in[:, 1:2], by_r_in[:, 0:1], -1.0)
        fma(by_r_in[:, 3:4], by_r_in[:, 1:2], s64[:])
        neg_tanh64 = column("neg_tanh64")
        fma(neg_tanh64[:], tanh[:], -1.0 / 64)
        by_r = column("by_r", 5)
        fma(by_r[:, 4:5], by_r_in[:, 3:4], neg_tanh64[:])
        coef = column("coef", 3)
        fma(coef[:, 2:3], s64[:], z[:])

        scratch = sb.tile([P, I + 8], F32, name="scratch", tag="val_scale_pool")
        r = scratch[:, I : I + 1]
        nc.vector.reciprocal(out=r, in_=z[:])
        neg_ta_a = column("neg_ta_a")
        nc.vector.scalar_tensor_tensor(
            out=scratch[:, 0:I], in0=ta[:], scalar=1.0, in1=neg_a[:], op0=ALU.mult, op1=ALU.mult, accum_out=neg_ta_a[:]
        )
        t = column("t")
        unused_t = wide("unused_t")
        nc.vector.scalar_tensor_tensor(
            out=unused_t[:], in0=ta[:], scalar=r, in1=p[:], op0=ALU.mult, op1=ALU.mult, accum_out=t[:]
        )
        fma(by_r[:, 0:4], by_r_in[:], r)
        k3, neg_k3, neg_r = by_r[:, 0:1], by_r[:, 1:2], by_r[:, 2:3]
        fma(coef[:, 0:2], by_r[:, 3:5], neg_ta_a[:])

        c_mean = column("c_mean")
        unused_c = wide("unused_c")
        nc.scalar.activation(out=unused_c[:], in_=c0[:], func=ACT.Copy, scale=1.0 / I, accum_out=c_mean[:])

        sx_beta = column("sx_beta", 2)
        fma(sx_beta[:, 1:2], t[:], neg_k3, coef[:, 0:1])
        x = wide("x")
        nc.scalar.activation(
            out=x[:], in_=ta[:], func=ACT.Identity, scale=k3, bias=sx_beta[:, 1:2], accum_out=sx_beta[:, 0:1]
        )

        m = column("m")
        unused_m = wide("unused_m")
        nc.vector.scalar_tensor_tensor(
            out=unused_m[:], in0=c0[:], scalar=r, in1=p[:], op0=ALU.mult, op1=ALU.mult, accum_out=m[:]
        )
        c1_nk = column("c1_nk", 2)
        nc.vector.scalar_tensor_tensor(
            out=c1_nk[:],
            in0=c_mean[:].to_broadcast([P, 2]),
            scalar=m[:],
            in1=coef[:, 1:3],
            op0=ALU.subtract,
            op1=ALU.mult,
        )
        c1, neg_kappa = c1_nk[:, 0:1], c1_nk[:, 1:2]
        q = wide("q")
        nc.vector.scalar_tensor_tensor(out=q[:], in0=c0[:], scalar=m[:], in1=p[:], op0=ALU.subtract, op1=ALU.mult)
        h = wide("h")
        sum_h = column("sum_h")
        nc.vector.scalar_tensor_tensor(
            out=h[:], in0=q[:], scalar=neg_kappa, in1=x[:], op0=ALU.subtract, op1=ALU.mult, accum_out=sum_h[:]
        )
        by_kappa = column("by_kappa", 2)
        fma(by_kappa[:], sx_beta[:], neg_kappa)
        k0 = column("k0")
        fma(k0[:], by_kappa[:, 0:1], s64[:], c1)

        gamma = column("gamma")
        nc.vector.tensor_scalar(
            out=gamma[:], in0=sum_h[:], scalar1=by_kappa[:, 0:1], scalar2=neg_r, op0=ALU.add, op1=ALU.mult
        )
        k5 = column("k5")
        fma(k5[:], sum_h[:], s64[:], k0[:])
        v_a = wide("v_a")
        fma(v_a[:], a[:], k5[:], by_kappa[:, 1:2])
        v_p = wide("v_p")
        nc.vector.scalar_tensor_tensor(out=v_p[:], in0=p[:], scalar=gamma[:], in1=h[:], op0=ALU.mult, op1=ALU.add)

        nc.vector.tensor_tensor(placed[:].indirect(offsets[:]), v_p[:], v_a[:], ALU.add)

        for n in range(len(OUT_EDGES) - 1):
            cols = slice(OUT_EDGES[n], OUT_EDGES[n + 1])
            total = sb.tile([P, cols.stop - cols.start], F32, name=f"total{n}")
            nc.vector.tensor_tensor(total[:], placed[:, cols], base_sb[:, cols], ALU.add)
            queue = nc.sync if n % 2 == 0 else nc.scalar
            queue.dma_start(out=out[:, cols], in_=total[:])
